import numpy as np, ml_dtypes
CORES = [10,14,66,70,74,78,82,86,90,94,106,110]
N = 12
T, CAP = 512, 192
def entries(a): return a.T.reshape(-1)
def pack(v, P): return np.ascontiguousarray(np.asarray(v, np.int32).reshape(-1, P).T)
def lists(rng, how):
    n = rng.integers(1, CAP + 1, N)
    if how == "none": n[rng.integers(N)] = 0; n[rng.integers(N)] = 0
    if how == "full": n[:] = CAP
    if how == "one": n[:] = 1
    if how == "void": n[:] = 0
    Kp = np.zeros((N, T), np.int32)
    for r in range(N): Kp[r, (np.arange(T - n[r], T) if how == "last" else rng.permutation(T)[:n[r]])] = 1
    return {"keep": np.stack([pack(Kp[r], 16) for r in range(N)])}
def setup_inputs(rng):
    return dict({"x": rng.standard_normal((N, 128, T), dtype=np.float32).astype(ml_dtypes.bfloat16)}, **lists(rng, "uniform"))
def setup_inputs_full(rng):
    d = setup_inputs(rng); d.update(lists(rng, "full"))
    for k in ("x",): d[k] = (d[k].astype(np.float32) * 1048576.0).astype(d[k].dtype)
    return d
def setup_inputs_last(rng):
    d = setup_inputs(rng); d.update(lists(rng, "last"))
    for k in ("x",): d[k] = (d[k].astype(np.float32) * (1 / 1024.0)).astype(d[k].dtype)
    return d
def setup_inputs_none(rng):
    d = setup_inputs(rng); d.update(lists(rng, "none"))
    return d
def setup_inputs_one(rng):
    d = setup_inputs(rng); d.update(lists(rng, "one"))
    return d
def setup_inputs_void(rng):
    d = setup_inputs(rng); d.update(lists(rng, "void"))
    return d
def check_inputs(x):
    bad = []
    if x["keep"].min() < 0 or x["keep"].max() >= 2: bad.append("keep out of range")
    if max(int(a.sum()) for a in x["keep"]) > CAP: bad.append("a rank keeps more than CAP")
    return bad
def reference(x, keep):
    kept = np.concatenate([x[r][:, entries(keep[r]) == 1] for r in range(N)], axis=1)
    y = np.zeros((128, N * CAP), x.dtype); y[:, :kept.shape[1]] = kept
    return {"y": np.broadcast_to(y, (N, 128, N * CAP))}

@@ -1,0 +1,240 @@
+from concourse.bass import DstId, RemoteDMATransfer
+from concourse.mybir import AluOpType, AxisListType, ActivationFunctionType
+
+N, TC, CAP = 12, 512, 192
+YW = N * CAP
+NQ = 4
+QW = YW // NQ
+
+SCRATCH = {
+    "xs": ("sbuf", [128, TC], "bfloat16"),
+    "cb": ("sbuf", [128, TC], "bfloat16"),
+    "land": ("sbuf", [128, 2 * YW], "bfloat16"),
+    "ysb": ("sbuf", [128, YW], "bfloat16"),
+    "kall": ("dram", [N, 128, 4], "int32"),
+    "kw": ("sbuf", [16, 32], "int32"),
+    "fl": ("sbuf", [96, 64], "int32"),
+    "ff": ("sbuf", [96, 64], "float32"),
+    "nf": ("sbuf", [96, 1], "float32"),
+    "nb": ("sbuf", [97, 1], "bfloat16"),
+    "qk": ("sbuf", [16, 128], "float32"),
+    "c16": ("sbuf", [16, 32], "int32"),
+    "ip": ("sbuf", [16, 144], "float32"),
+    "tv": ("sbuf", [96, 208], "float32"),
+    "eb": ("sbuf", [16, 128], "bfloat16"),
+    "e32": ("sbuf", [16, 128], "float32"),
+    "w3": ("sbuf", [16, 128], "bfloat16"),
+    "e2": ("sbuf", [16, 128], "bfloat16"),
+    "uu": ("sbuf", [16, 128], "bfloat16"),
+    "w1": ("sbuf", [16, 128], "bfloat16"),
+    "w2": ("sbuf", [16, 128], "bfloat16"),
+    "kbp": ("sbuf", [16, 33], "bfloat16"),
+    "kcp": ("sbuf", [16, 33], "bfloat16"),
+    "m16": ("sbuf", [128, 32], "float32"),
+    "of": ("sbuf", [128, 32], "float32"),
+    "ou": ("sbuf", [128, 32], "uint16"),
+    "tall": ("sbuf", [97, 208], "bfloat16"),
+    "tdd": ("sbuf", [97, 192], "bfloat16"),
+    "eq": ("sbuf", [128, 128], "bfloat16"),
+    "jw": ("sbuf", [128, 144], "float32"),
+    "r0": ("sbuf", [128, 144], "bfloat16"),
+    "r1": ("sbuf", [64, 144], "bfloat16"),
+    "gf": ("sbuf", [128, 144], "float32"),
+    "gu": ("sbuf", [128, 144], "uint16"),
+    "psd": ("psum", [128, 512], "float32"),
+    "pse": ("psum", [128, 512], "float32"),
+    "psj": ("psum", [128, 512], "float32"),
+    "pso": ("psum", [128, 512], "float32"),
+    "psg": ("psum", [128, 512], "float32"),
+}
+SEMAPHORES = (["kd", "kwl", "xl", "fld", "fa", "fw", "loc", "sts", "stc",
+               "gq", "gj", "gt", "vm", "vc1", "vc2", "vc3", "vk", "vs1", "vs2", "vsc", "vown", "vz",
+               "vt1", "vt2", "vq", "vf1", "vf2", "vf3", "vr", "vg1", "vg2", "te", "td", "to", "tg"]
+              + ["a%d" % r for r in range(N)] + ["y%d" % q for q in range(NQ)])
+
+
+def _bits(mask):
+    return [b for b in range(16) if (mask >> b) & 1]
+
+
+def _mask_of(bits):
+    m = 0
+    for b in bits:
+        m |= 1 << b
+    return m
+
+
+def rank_program(g, core, T, topo):
+    rank = T.rank_of(core)
+    if rank is None:
+        return
+    S = T.sem
+    V, PE, SC, SY = g.vector, g.tensor, g.scalar, g.sync
+    A = AluOpType
+    cores = list(T.cores)
+
+    chips = []
+    for c in cores:
+        if topo.chip(c) not in chips:
+            chips.append(topo.chip(c))
+    nch = len(chips)
+    ci = chips.index(topo.chip(core))
+    sib = [c for c in cores if topo.chip(c) == topo.chip(core) and c != core][0]
+
+    def same_die(chip_no, die_no):
+        return [c for c in cores if topo.chip(c) == chip_no and topo.die(c) == die_no][0]
+
+    outs = [same_die(chips[(ci + k) % nch], topo.die(core)) for k in range(1, nch)]
+    ins = [same_die(chips[(ci - k) % nch], topo.die(core)) for k in range(1, nch)]
+    for c in outs + [sib]:
+        assert topo.may_write(core, c)
+    far = topo.mask(core, sib)
+    for c in outs:
+        far &= topo.mask(core, c)
+    near = topo.mask(core, sib) & ~far
+    nfar, nnear = len(_bits(far)), len(_bits(near))
+    fmask = _mask_of(_bits(far)[:4])
+    nfm = len(_bits(fmask))
+
+    def did(c):
+        rid, pid, _ = topo.addr(c)
+        return DstId(rid=rid, pnc=pid)
+
+    def slot(r):
+        return T.land[:, CAP * r:CAP * (r + 1)]
+
+    SY.dma_start(T.kw[:], T.keep[:]).then_inc(S.kwl, 16)
+    SY.dma_start(T.kall[rank], T.keep[:]).then_inc(S.kd, 16)
+    SC.dma_start(T.xs[:], T.x[:]).then_inc(S.xl, 16)
+
+    g.iota(T.qk[:], [[0, 8], [1, 16]], 0, -1, allow_small_or_imprecise_dtypes=True).then_inc(S.gq, 1)
+    g.iota(T.kcp[:, 0:1], [[0, 1]], 15, -1, allow_small_or_imprecise_dtypes=True).then_inc(S.gq, 1)
+    g.iota(T.c16[:], [[-16, 32]], 496, 0).then_inc(S.gq, 1)
+    g.iota(T.ip[:], [[16, 144]], 0, 1, allow_small_or_imprecise_dtypes=True).then_inc(S.gj, 1)
+    g.iota(T.tv[:], [[8, 13], [0, 16]], 0, -1, allow_small_or_imprecise_dtypes=True).then_inc(S.gt, 1)
+
+    g.wait_ge(S.kd, 16)
+    others = [c for c in cores if c != core]
+    g.remote_dma_fused([RemoteDMATransfer(dst_ids=[did(c) for c in others], dma_engine_mask=fmask, remote_sem=S.fa,
+                                          srcs=[T.kall[rank]], dsts=[T.kall[rank] for c in others])],
+                       local_sem=S.loc)
+    g.wait_ge(S.vsc, 1)
+    g.remote_dma_fused([
+        RemoteDMATransfer(dst_ids=[did(c) for c in outs], dma_engine_mask=far, remote_sem=S["a%d" % rank],
+                          srcs=[T.cb[:, 0:CAP]], dsts=[slot(rank) for c in outs]),
+        RemoteDMATransfer(dst_ids=[did(sib)], dma_engine_mask=near, remote_sem=S.fw,
+                          srcs=[T.cb[:, 0:CAP]], dsts=[slot(rank)]),
+    ], local_sem=S.loc)
+    srid, spid, _ = topo.addr(sib)
+    for c in ins:
+        r = T.rank_of(c)
+        g.wait_ge(S["a%d" % r], nfar)
+        g.remote_dma(slot(r), slot(r), S.fw, S.loc, spid, srid, near)
+    g.wait_ge(S.loc, nfm + nfar + nnear + nnear * len(ins))
+
+    V.memset(T.kbp[:, 0:1], 0.0).then_inc(S.vm, 1)
+    V.memset(T.m16[:], -16.0).then_inc(S.vm, 1)
+    V.wait_ge(S.gq, 3)
+    V.tensor_scalar(T.eb[:], T.qk[:], 0.0, None, A.is_equal).then_inc(S.vc1, 1)
+    V.tensor_scalar(T.e32[:], T.qk[:], 0.0, None, A.is_equal).then_inc(S.vc1, 1)
+    V.tensor_scalar(T.w3[:], T.qk[:], 0.0, -1.0, A.is_equal, A.mult).then_inc(S.vc1, 1)
+    V.tensor_scalar(T.e2[:], T.qk[:], 0.0, T.kcp[:, 0:1], A.is_equal, A.mult).then_inc(S.vc1, 1)
+    V.tensor_scalar(T.uu[:], T.qk[:], 0.0, None, A.is_gt).then_inc(S.vc1, 1)
+    V.wait_ge(S.vc1, 5)
+    V.tensor_tensor(T.w1[:], T.uu[:], T.e2[:], A.subtract).then_inc(S.vc2, 1)
+    V.wait_ge(S.vc2, 1)
+    V.tensor_scalar(T.w2[:], T.w1[:], -1.0, 1.0, A.mult, A.add).then_inc(S.vc3, 1)
+    V.wait_ge(S.kwl, 16)
+    V.tensor_copy(T.kbp[:, 1:33], T.kw[:]).then_inc(S.vk, 1)
+    V.tensor_tensor(T.kcp[:, 1:33], T.kw[:], T.c16[:], A.mult).then_inc(S.vk, 1)
+    V.wait_ge(S.td, 4)
+    V.wait_ge(S.vm, 2)
+    V.tensor_tensor_scan(T.of[:], T.psd[:, 0:32], T.m16[:], 512.0, A.add, A.add).then_inc(S.vs1, 1)
+    V.wait_ge(S.vs1, 1)
+    V.tensor_copy(T.ou[:], T.of[:]).then_inc(S.vs2, 1)
+    V.wait_ge(S.vs2, 1)
+    V.wait_ge(S.xl, 16)
+    V.tensor_copy(T.cb[:, 0:TC].indirect(T.ou[:, 0:32]), T.xs[:]).then_inc(S.vsc, 1)
+    V.wait_ge(S.vsc, 1)
+    V.tensor_copy(slot(rank), T.cb[:, 0:CAP]).then_inc(S.vown, 1)
+    V.memset(T.land[:, YW:2 * YW], 0.0).then_inc(S.vz, 1)
+    V.memset(T.nb[96:97, 0:1], 1.0).then_inc(S.vz, 1)
+    V.memset(T.tall[96:97, :], 0.0).then_inc(S.vz, 1)
+    V.memset(T.tdd[96:97, :], 192.0).then_inc(S.vz, 1)
+    V.wait_ge(S.gt, 1)
+    V.tensor_scalar(T.tall[0:96, :], T.tv[:], 0.0, None, A.is_gt).then_inc(S.vt1, 1)
+    V.wait_ge(S.vt1, 1)
+    V.tensor_tensor(T.tdd[0:96, :], T.tall[0:96, 0:192], T.tall[0:96, 16:208], A.subtract).then_inc(S.vt2, 1)
+    V.wait_ge(S.te, 2)
+    V.tensor_copy(T.eq[:], T.pse[:, 0:128]).then_inc(S.vq, 1)
+    V.tensor_copy(T.jw[:], T.psj[:, 0:144]).then_inc(S.vq, 1)
+    V.wait_ge(S.fld, 16)
+    V.tensor_copy(T.ff[:], T.fl[:]).then_inc(S.vf1, 1)
+    V.wait_ge(S.vf1, 1)
+    V.tensor_reduce(T.nf[:], T.ff[:], AxisListType.X, A.add).then_inc(S.vf2, 1)
+    V.wait_ge(S.vf2, 1)
+    V.tensor_copy(T.nb[0:96, 0:1], T.nf[:]).then_inc(S.vf3, 1)
+    V.wait_ge(S.to, 4)
+    V.wait_ge(S.vq, 2)
+    V.tensor_scalar(T.r0[:], T.jw[:], T.pso[:, 0:1], T.pso[:, 1:2], A.is_ge, A.mult).then_inc(S.vr, 1)
+    V.tensor_scalar(T.r1[:], T.jw[0:64, :], T.pso[0:64, 2:3], T.pso[0:64, 3:4], A.is_ge, A.mult).then_inc(S.vr, 1)
+    V.wait_ge(S.tg, 2)
+    V.tensor_tensor(T.gf[:], T.psg[:, 0:144], T.jw[:], A.add).then_inc(S.vg1, 1)
+    V.wait_ge(S.vg1, 1)
+    V.tensor_copy(T.gu[:], T.gf[:]).then_inc(S.vg2, 1)
+
+    PE.wait_ge(S.vc1, 5)
+    PE.matmul(T.pse[:, 0:128], T.eb[:], T.eb[:], True, True).then_inc(S.te, 1)
+    PE.wait_ge(S.gj, 1)
+    PE.matmul(T.psj[:, 0:144], T.e32[:], T.ip[:], True, True).then_inc(S.te, 1)
+    PE.wait_ge(S.vc2, 1)
+    PE.wait_ge(S.vc3, 1)
+    PE.wait_ge(S.vm, 2)
+    PE.wait_ge(S.gq, 3)
+    PE.wait_ge(S.vk, 2)
+    PE.matmul(T.psd[:, 0:32], T.w1[:], T.kbp[:, 1:33], True, False).then_inc(S.td, 1)
+    PE.matmul(T.psd[:, 0:32], T.w2[:], T.kbp[:, 0:32], False, False).then_inc(S.td, 1)
+    PE.matmul(T.psd[:, 0:32], T.w3[:], T.kcp[:, 1:33], False, False).then_inc(S.td, 1)
+    PE.matmul(T.psd[:, 0:32], T.eb[:], T.kcp[:, 0:32], False, True).then_inc(S.td, 1)
+    PE.wait_ge(S.vz, 4)
+    PE.wait_ge(S.vt1, 1)
+    PE.wait_ge(S.vt2, 1)
+    PE.wait_ge(S.vf3, 1)
+    PE.matmul(T.pso[:, 0:1], T.tall[:, 16:144], T.nb[:], True, True).then_inc(S.to, 1)
+    PE.matmul(T.pso[:, 1:2], T.tdd[:, 0:128], T.nb[:], True, True).then_inc(S.to, 1)
+    PE.matmul(T.pso[0:64, 2:3], T.tall[:, 144:208], T.nb[:], True, True).then_inc(S.to, 1)
+    PE.matmul(T.pso[0:64, 3:4], T.tdd[:, 128:192], T.nb[:], True, True).then_inc(S.to, 1)
+    PE.wait_ge(S.vq, 2)
+    PE.wait_ge(S.vr, 2)
+    PE.matmul(T.psg[:, 0:144], T.eq[:], T.r0[:], True, False).then_inc(S.tg, 1)
+    PE.matmul(T.psg[:, 0:144], T.eq[0:64, :], T.r1[:], False, True).then_inc(S.tg, 1)
+
+    SY.wait_ge(S.fa, nfm * len(others))
+    SY.wait_ge(S.kd, 16)
+    SY.dma_start(T.fl[:], T.kall[:]).then_inc(S.fld, 16)
+
+    def all_here(q):
+        q.wait_ge(S.vg2, 1)
+        q.wait_ge(S.vown, 1)
+        q.wait_ge(S.vz, 4)
+        for c in ins:
+            q.wait_ge(S["a%d" % T.rank_of(c)], nfar)
+        q.wait_ge(S.fw, nnear * (len(ins) + 1))
+
+    def src(p):
+        return T.land[:, 0:2 * YW].indirect(T.gu[:, p * QW // 16:(p + 1) * QW // 16])
+
+    all_here(V)
+    all_here(SC)
+    for p in range(NQ):
+        piece = T.ysb[:, p * QW:(p + 1) * QW]
+        if p % 2 == 0:
+            V.tensor_copy(piece, src(p)).then_inc(S["y%d" % p], 1)
+            SY.wait_ge(S["y%d" % p], 1)
+            SY.dma_start(T.y[:, p * QW:(p + 1) * QW], piece).then_inc(S.sts, 16)
+        else:
+            SC.activation(piece, src(p), ActivationFunctionType.Copy).then_inc(S["y%d" % p], 1)
+            SC.wait_ge(S["y%d" % p], 1)
+            SC.dma_start(T.y[:, p * QW:(p + 1) * QW], piece).then_inc(S.stc, 16)
+    SY.wait_ge(S.sts, 16 * (NQ // 2))
+    SC.wait_ge(S.stc, 16 * (NQ // 2))

@@ -3,13 +3,14 @@ from concourse.mybir import AluOpType, AxisListType, ActivationFunctionType
 
 N, TC, CAP = 12, 512, 192
 YW = N * CAP
+ZW = 16
 NQ = 4
 QW = YW // NQ
 
 SCRATCH = {
     "xs": ("sbuf", [128, TC], "bfloat16"),
     "cb": ("sbuf", [128, TC], "bfloat16"),
-    "land": ("sbuf", [128, 2 * YW], "bfloat16"),
+    "land": ("sbuf", [128, YW + ZW], "bfloat16"),
     "ysb": ("sbuf", [128, YW], "bfloat16"),
     "kall": ("dram", [N, 128, 4], "int32"),
     "kw": ("sbuf", [16, 32], "int32"),
@@ -17,10 +18,12 @@ SCRATCH = {
     "ff": ("sbuf", [96, 64], "float32"),
     "nf": ("sbuf", [96, 1], "float32"),
     "nb": ("sbuf", [97, 1], "bfloat16"),
-    "qk": ("sbuf", [16, 128], "float32"),
+    "qk": ("sbuf", [16, 128], "bfloat16"),
+    "z32": ("sbuf", [16, 32], "float32"),
+    "c16f": ("sbuf", [16, 32], "float32"),
     "c16": ("sbuf", [16, 32], "int32"),
     "ip": ("sbuf", [16, 144], "float32"),
-    "tv": ("sbuf", [96, 208], "float32"),
+    "tv": ("sbuf", [96, 208], "bfloat16"),
     "eb": ("sbuf", [16, 128], "bfloat16"),
     "e32": ("sbuf", [16, 128], "float32"),
     "w3": ("sbuf", [16, 128], "bfloat16"),
@@ -39,17 +42,18 @@ SCRATCH = {
     "jw": ("sbuf", [128, 144], "float32"),
     "r0": ("sbuf", [128, 144], "bfloat16"),
     "r1": ("sbuf", [64, 144], "bfloat16"),
-    "gf": ("sbuf", [128, 144], "float32"),
     "gu": ("sbuf", [128, 144], "uint16"),
     "psd": ("psum", [128, 512], "float32"),
     "pse": ("psum", [128, 512], "float32"),
     "psj": ("psum", [128, 512], "float32"),
     "pso": ("psum", [128, 512], "float32"),
+    "pso2": ("psum", [128, 512], "float32"),
     "psg": ("psum", [128, 512], "float32"),
 }
 SEMAPHORES = (["kd", "kwl", "xl", "fld", "fa", "fw", "loc", "sts", "stc",
-               "gq", "gj", "gt", "vm", "vc1", "vc2", "vc3", "vk", "vs1", "vs2", "vsc", "vown", "vz",
-               "vt1", "vt2", "vq", "vf1", "vf2", "vf3", "vr", "vg1", "vg2", "te", "td", "to", "tg"]
+               "gq", "gj", "gt", "vm", "vc0a", "vc0b", "vc1", "vc2", "vc3", "vk", "vs1", "vs2", "vsc", "vown", "vz",
+               "vt1", "vt2", "vf1", "vf2", "vf3", "vr0", "vr1", "vg2", "se", "sq", "sj",
+               "te1", "te2", "td", "to1", "to2", "tg"]
               + ["a%d" % r for r in range(N)] + ["y%d" % q for q in range(NQ)])
 
 
@@ -71,6 +75,7 @@ def rank_program(g, core, T, topo):
     S = T.sem
     V, PE, SC, SY = g.vector, g.tensor, g.scalar, g.sync
     A = AluOpType
+    CP = ActivationFunctionType.Copy
     cores = list(T.cores)
 
     chips = []
@@ -84,17 +89,24 @@ def rank_program(g, core, T, topo):
     def same_die(chip_no, die_no):
         return [c for c in cores if topo.chip(c) == chip_no and topo.die(c) == die_no][0]
 
+    def hops(c):
+        a, b = topo.chip(core), topo.chip(c)
+        if a == b:
+            return 0
+        return 1 if (topo.mates(a, b) or topo.same_plane(a, b)) else 2
+
     outs = [same_die(chips[(ci + k) % nch], topo.die(core)) for k in range(1, nch)]
     ins = [same_die(chips[(ci - k) % nch], topo.die(core)) for k in range(1, nch)]
-    for c in outs + [sib]:
+    others = sorted([c for c in cores if c != core], key=lambda c: -hops(c))
+    for c in others:
         assert topo.may_write(core, c)
     far = topo.mask(core, sib)
     for c in outs:
         far &= topo.mask(core, c)
     near = topo.mask(core, sib) & ~far
     nfar, nnear = len(_bits(far)), len(_bits(near))
-    fmask = _mask_of(_bits(far)[:4])
-    nfm = len(_bits(fmask))
+    fbits = _bits(far)[::2]
+    nfb = len(fbits)
 
     def did(c):
         rid, pid, _ = topo.addr(c)
@@ -103,61 +115,59 @@ def rank_program(g, core, T, topo):
     def slot(r):
         return T.land[:, CAP * r:CAP * (r + 1)]
 
-    SY.dma_start(T.kw[:], T.keep[:]).then_inc(S.kwl, 16)
     SY.dma_start(T.kall[rank], T.keep[:]).then_inc(S.kd, 16)
+    SY.dma_start(T.kw[:], T.keep[:]).then_inc(S.kwl, 16)
     SC.dma_start(T.xs[:], T.x[:]).then_inc(S.xl, 16)
 
     g.iota(T.qk[:], [[0, 8], [1, 16]], 0, -1, allow_small_or_imprecise_dtypes=True).then_inc(S.gq, 1)
-    g.iota(T.kcp[:, 0:1], [[0, 1]], 15, -1, allow_small_or_imprecise_dtypes=True).then_inc(S.gq, 1)
-    g.iota(T.c16[:], [[-16, 32]], 496, 0).then_inc(S.gq, 1)
+    g.wait_ge(S.kd, 16)
+    g.remote_dma_fused([RemoteDMATransfer(dst_ids=[did(c) for c in others[i::nfb]], dma_engine_mask=_mask_of([fbits[i]]),
+                                          remote_sem=S.fa, srcs=[T.kall[rank]],
+                                          dsts=[T.kall[rank] for c in others[i::nfb]])
+                        for i in range(nfb)], local_sem=S.loc)
     g.iota(T.ip[:], [[16, 144]], 0, 1, allow_small_or_imprecise_dtypes=True).then_inc(S.gj, 1)
     g.iota(T.tv[:], [[8, 13], [0, 16]], 0, -1, allow_small_or_imprecise_dtypes=True).then_inc(S.gt, 1)
-
-    g.wait_ge(S.kd, 16)
-    others = [c for c in cores if c != core]
-    g.remote_dma_fused([RemoteDMATransfer(dst_ids=[did(c) for c in others], dma_engine_mask=fmask, remote_sem=S.fa,
-                                          srcs=[T.kall[rank]], dsts=[T.kall[rank] for c in others])],
-                       local_sem=S.loc)
     g.wait_ge(S.vsc, 1)
-    g.remote_dma_fused([
-        RemoteDMATransfer(dst_ids=[did(c) for c in outs], dma_engine_mask=far, remote_sem=S["a%d" % rank],
-                          srcs=[T.cb[:, 0:CAP]], dsts=[slot(rank) for c in outs]),
-        RemoteDMATransfer(dst_ids=[did(sib)], dma_engine_mask=near, remote_sem=S.fw,
-                          srcs=[T.cb[:, 0:CAP]], dsts=[slot(rank)]),
-    ], local_sem=S.loc)
+    g.remote_dma_fused([RemoteDMATransfer(dst_ids=[did(c) for c in outs], dma_engine_mask=far,
+                                          remote_sem=S["a%d" % rank],
+                                          srcs=[T.cb[:, 0:CAP]], dsts=[slot(rank) for c in outs])], local_sem=S.loc)
     srid, spid, _ = topo.addr(sib)
+    g.remote_dma(slot(rank), T.cb[:, 0:CAP], S.fw, S.loc, spid, srid, near)
     for c in ins:
         r = T.rank_of(c)
         g.wait_ge(S["a%d" % r], nfar)
         g.remote_dma(slot(r), slot(r), S.fw, S.loc, spid, srid, near)
-    g.wait_ge(S.loc, nfm + nfar + nnear + nnear * len(ins))
+    g.wait_ge(S.loc, nfb + nfar + nnear + nnear * len(ins))
 
     V.memset(T.kbp[:, 0:1], 0.0).then_inc(S.vm, 1)
     V.memset(T.m16[:], -16.0).then_inc(S.vm, 1)
-    V.wait_ge(S.gq, 3)
+    V.memset(T.z32[:], 0.0).then_inc(S.vm, 1)
+    V.wait_ge(S.vm, 3)
+    V.tensor_tensor_scan(T.c16f[:], T.m16[0:16, :], T.z32[:], 512.0, A.add, A.add).then_inc(S.vc0a, 1)
+    V.wait_ge(S.vc0a, 1)
+    V.tensor_copy(T.c16[:], T.c16f[:]).then_inc(S.vc0b, 1)
+    V.wait_ge(S.gq, 1)
+    V.tensor_copy(T.kcp[:, 0:1], T.qk[:, 15:16]).then_inc(S.vc1, 1)
     V.tensor_scalar(T.eb[:], T.qk[:], 0.0, None, A.is_equal).then_inc(S.vc1, 1)
-    V.tensor_scalar(T.e32[:], T.qk[:], 0.0, None, A.is_equal).then_inc(S.vc1, 1)
     V.tensor_scalar(T.w3[:], T.qk[:], 0.0, -1.0, A.is_equal, A.mult).then_inc(S.vc1, 1)
-    V.tensor_scalar(T.e2[:], T.qk[:], 0.0, T.kcp[:, 0:1], A.is_equal, A.mult).then_inc(S.vc1, 1)
+    V.tensor_scalar(T.e2[:], T.qk[:], 0.0, T.qk[:, 15:16], A.is_equal, A.mult).then_inc(S.vc1, 1)
     V.tensor_scalar(T.uu[:], T.qk[:], 0.0, None, A.is_gt).then_inc(S.vc1, 1)
     V.wait_ge(S.vc1, 5)
     V.tensor_tensor(T.w1[:], T.uu[:], T.e2[:], A.subtract).then_inc(S.vc2, 1)
     V.wait_ge(S.vc2, 1)
     V.tensor_scalar(T.w2[:], T.w1[:], -1.0, 1.0, A.mult, A.add).then_inc(S.vc3, 1)
+    V.wait_ge(S.vc0b, 1)
     V.wait_ge(S.kwl, 16)
     V.tensor_copy(T.kbp[:, 1:33], T.kw[:]).then_inc(S.vk, 1)
     V.tensor_tensor(T.kcp[:, 1:33], T.kw[:], T.c16[:], A.mult).then_inc(S.vk, 1)
     V.wait_ge(S.td, 4)
-    V.wait_ge(S.vm, 2)
     V.tensor_tensor_scan(T.of[:], T.psd[:, 0:32], T.m16[:], 512.0, A.add, A.add).then_inc(S.vs1, 1)
     V.wait_ge(S.vs1, 1)
     V.tensor_copy(T.ou[:], T.of[:]).then_inc(S.vs2, 1)
     V.wait_ge(S.vs2, 1)
     V.wait_ge(S.xl, 16)
     V.tensor_copy(T.cb[:, 0:TC].indirect(T.ou[:, 0:32]), T.xs[:]).then_inc(S.vsc, 1)
-    V.wait_ge(S.vsc, 1)
-    V.tensor_copy(slot(rank), T.cb[:, 0:CAP]).then_inc(S.vown, 1)
-    V.memset(T.land[:, YW:2 * YW], 0.0).then_inc(S.vz, 1)
+    V.memset(T.land[:, YW:YW + ZW], 0.0).then_inc(S.vz, 1)
     V.memset(T.nb[96:97, 0:1], 1.0).then_inc(S.vz, 1)
     V.memset(T.tall[96:97, :], 0.0).then_inc(S.vz, 1)
     V.memset(T.tdd[96:97, :], 192.0).then_inc(S.vz, 1)
@@ -165,51 +175,58 @@ def rank_program(g, core, T, topo):
     V.tensor_scalar(T.tall[0:96, :], T.tv[:], 0.0, None, A.is_gt).then_inc(S.vt1, 1)
     V.wait_ge(S.vt1, 1)
     V.tensor_tensor(T.tdd[0:96, :], T.tall[0:96, 0:192], T.tall[0:96, 16:208], A.subtract).then_inc(S.vt2, 1)
-    V.wait_ge(S.te, 2)
-    V.tensor_copy(T.eq[:], T.pse[:, 0:128]).then_inc(S.vq, 1)
-    V.tensor_copy(T.jw[:], T.psj[:, 0:144]).then_inc(S.vq, 1)
     V.wait_ge(S.fld, 16)
     V.tensor_copy(T.ff[:], T.fl[:]).then_inc(S.vf1, 1)
     V.wait_ge(S.vf1, 1)
     V.tensor_reduce(T.nf[:], T.ff[:], AxisListType.X, A.add).then_inc(S.vf2, 1)
     V.wait_ge(S.vf2, 1)
     V.tensor_copy(T.nb[0:96, 0:1], T.nf[:]).then_inc(S.vf3, 1)
-    V.wait_ge(S.to, 4)
-    V.wait_ge(S.vq, 2)
-    V.tensor_scalar(T.r0[:], T.jw[:], T.pso[:, 0:1], T.pso[:, 1:2], A.is_ge, A.mult).then_inc(S.vr, 1)
-    V.tensor_scalar(T.r1[:], T.jw[0:64, :], T.pso[0:64, 2:3], T.pso[0:64, 3:4], A.is_ge, A.mult).then_inc(S.vr, 1)
-    V.wait_ge(S.tg, 2)
-    V.tensor_tensor(T.gf[:], T.psg[:, 0:144], T.jw[:], A.add).then_inc(S.vg1, 1)
-    V.wait_ge(S.vg1, 1)
-    V.tensor_copy(T.gu[:], T.gf[:]).then_inc(S.vg2, 1)
+    V.wait_ge(S.sj, 1)
+    V.wait_ge(S.to1, 2)
+    V.tensor_scalar(T.r0[:], T.jw[:], T.pso[:, 0:1], T.pso[:, 1:2], A.is_ge, A.mult).then_inc(S.vr0, 1)
+    V.wait_ge(S.to2, 2)
+    V.tensor_scalar(T.r1[:], T.jw[0:64, :], T.pso2[0:64, 0:1], T.pso2[0:64, 1:2], A.is_ge, A.mult).then_inc(S.vr1, 1)
+    V.wait_ge(S.tg, 3)
+    V.tensor_scalar(T.gu[:], T.psg[:, 0:144], float(YW), None, A.min).then_inc(S.vg2, 1)
+
+    SC.wait_ge(S.vc1, 5)
+    SC.activation(T.e32[:], T.eb[:], CP).then_inc(S.se, 1)
+    SC.wait_ge(S.te1, 1)
+    SC.activation(T.eq[:], T.pse[:, 0:128], CP).then_inc(S.sq, 1)
+    SC.wait_ge(S.te2, 1)
+    SC.activation(T.jw[:], T.psj[:, 0:144], CP).then_inc(S.sj, 1)
+    SC.wait_ge(S.vsc, 1)
+    SC.activation(slot(rank), T.cb[:, 0:CAP], CP).then_inc(S.vown, 1)
 
     PE.wait_ge(S.vc1, 5)
-    PE.matmul(T.pse[:, 0:128], T.eb[:], T.eb[:], True, True).then_inc(S.te, 1)
-    PE.wait_ge(S.gj, 1)
-    PE.matmul(T.psj[:, 0:144], T.e32[:], T.ip[:], True, True).then_inc(S.te, 1)
+    PE.matmul(T.pse[:, 0:128], T.eb[:], T.eb[:], True, True).then_inc(S.te1, 1)
     PE.wait_ge(S.vc2, 1)
     PE.wait_ge(S.vc3, 1)
-    PE.wait_ge(S.vm, 2)
-    PE.wait_ge(S.gq, 3)
+    PE.wait_ge(S.vm, 3)
     PE.wait_ge(S.vk, 2)
     PE.matmul(T.psd[:, 0:32], T.w1[:], T.kbp[:, 1:33], True, False).then_inc(S.td, 1)
     PE.matmul(T.psd[:, 0:32], T.w2[:], T.kbp[:, 0:32], False, False).then_inc(S.td, 1)
     PE.matmul(T.psd[:, 0:32], T.w3[:], T.kcp[:, 1:33], False, False).then_inc(S.td, 1)
     PE.matmul(T.psd[:, 0:32], T.eb[:], T.kcp[:, 0:32], False, True).then_inc(S.td, 1)
+    PE.wait_ge(S.se, 1)
+    PE.wait_ge(S.gj, 1)
+    PE.matmul(T.psj[:, 0:144], T.e32[:], T.ip[:], True, True).then_inc(S.te2, 1)
+    PE.matmul(T.psg[:, 0:144], T.e32[:], T.ip[:], True, False).then_inc(S.tg, 1)
     PE.wait_ge(S.vz, 4)
     PE.wait_ge(S.vt1, 1)
     PE.wait_ge(S.vt2, 1)
     PE.wait_ge(S.vf3, 1)
-    PE.matmul(T.pso[:, 0:1], T.tall[:, 16:144], T.nb[:], True, True).then_inc(S.to, 1)
-    PE.matmul(T.pso[:, 1:2], T.tdd[:, 0:128], T.nb[:], True, True).then_inc(S.to, 1)
-    PE.matmul(T.pso[0:64, 2:3], T.tall[:, 144:208], T.nb[:], True, True).then_inc(S.to, 1)
-    PE.matmul(T.pso[0:64, 3:4], T.tdd[:, 128:192], T.nb[:], True, True).then_inc(S.to, 1)
-    PE.wait_ge(S.vq, 2)
-    PE.wait_ge(S.vr, 2)
-    PE.matmul(T.psg[:, 0:144], T.eq[:], T.r0[:], True, False).then_inc(S.tg, 1)
+    PE.matmul(T.pso[:, 0:1], T.tall[:, 16:144], T.nb[:], True, True).then_inc(S.to1, 1)
+    PE.matmul(T.pso[:, 1:2], T.tdd[:, 0:128], T.nb[:], True, True).then_inc(S.to1, 1)
+    PE.matmul(T.pso2[0:64, 0:1], T.tall[:, 144:208], T.nb[:], True, True).then_inc(S.to2, 1)
+    PE.matmul(T.pso2[0:64, 1:2], T.tdd[:, 128:192], T.nb[:], True, True).then_inc(S.to2, 1)
+    PE.wait_ge(S.sq, 1)
+    PE.wait_ge(S.vr0, 1)
+    PE.matmul(T.psg[:, 0:144], T.eq[:], T.r0[:], False, False).then_inc(S.tg, 1)
+    PE.wait_ge(S.vr1, 1)
     PE.matmul(T.psg[:, 0:144], T.eq[0:64, :], T.r1[:], False, True).then_inc(S.tg, 1)
 
-    SY.wait_ge(S.fa, nfm * len(others))
+    SY.wait_ge(S.fa, len(others))
     SY.wait_ge(S.kd, 16)
     SY.dma_start(T.fl[:], T.kall[:]).then_inc(S.fld, 16)
 
@@ -222,7 +239,7 @@ def rank_program(g, core, T, topo):
         q.wait_ge(S.fw, nnear * (len(ins) + 1))
 
     def src(p):
-        return T.land[:, 0:2 * YW].indirect(T.gu[:, p * QW // 16:(p + 1) * QW // 16])
+        return T.land[:, 0:YW + ZW].indirect(T.gu[:, p * QW // 16:(p + 1) * QW // 16])
 
     all_here(V)
     all_here(SC)
@@ -233,7 +250,7 @@ def rank_program(g, core, T, topo):
             SY.wait_ge(S["y%d" % p], 1)
             SY.dma_start(T.y[:, p * QW:(p + 1) * QW], piece).then_inc(S.sts, 16)
         else:
-            SC.activation(piece, src(p), ActivationFunctionType.Copy).then_inc(S["y%d" % p], 1)
+            SC.activation(piece, src(p), CP).then_inc(S["y%d" % p], 1)
             SC.wait_ge(S["y%d" % p], 1)
             SC.dma_start(T.y[:, p * QW:(p + 1) * QW], piece).then_inc(S.stc, 16)
     SY.wait_ge(S.sts, 16 * (NQ // 2))

@@ -4,8 +4,8 @@ from concourse.mybir import AluOpType, AxisListType, ActivationFunctionType
 N, TC, CAP = 12, 512, 192
 YW = N * CAP
 ZW = 16
-NQ = 4
-QW = YW // NQ
+RW = [320, 512, 320]
+NQ = 2 * len(RW)
 
 SCRATCH = {
     "xs": ("sbuf", [128, TC], "bfloat16"),
@@ -28,10 +28,10 @@ SCRATCH = {
     "e32": ("sbuf", [16, 128], "float32"),
     "w3": ("sbuf", [16, 128], "bfloat16"),
     "e2": ("sbuf", [16, 128], "bfloat16"),
-    "uu": ("sbuf", [16, 128], "bfloat16"),
-    "w1": ("sbuf", [16, 128], "bfloat16"),
-    "w2": ("sbuf", [16, 128], "bfloat16"),
+    "uun": ("sbuf", [16, 128], "bfloat16"),
+    "on": ("sbuf", [16, 128], "bfloat16"),
     "kbp": ("sbuf", [16, 33], "bfloat16"),
+    "dn": ("sbuf", [16, 32], "bfloat16"),
     "kcp": ("sbuf", [16, 33], "bfloat16"),
     "m16": ("sbuf", [128, 32], "float32"),
     "of": ("sbuf", [128, 32], "float32"),
@@ -50,9 +50,9 @@ SCRATCH = {
     "pso2": ("psum", [128, 512], "float32"),
     "psg": ("psum", [128, 512], "float32"),
 }
-SEMAPHORES = (["kd", "kwl", "xl", "fld", "fa", "fw", "loc", "sts", "stc",
-               "gq", "gj", "gt", "vm", "vc0a", "vc0b", "vc1", "vc2", "vc3", "vk", "vs1", "vs2", "vsc", "vown", "vz",
-               "vt1", "vt2", "vf1", "vf2", "vf3", "vr0", "vr1", "vg2", "se", "sq", "sj",
+SEMAPHORES = (["kd", "kwl", "xl", "fld", "fa", "fw", "loc", "sts",
+               "gq", "gj", "gt", "vm", "vc0a", "vc0b", "vc1", "von", "vdn", "vk", "vk2", "vs1", "vs2", "vsc", "vown",
+               "vz", "vt1", "vt2", "vf1", "vf2", "vf3", "vr0", "vr1", "vg2", "se", "sq", "sj",
                "te1", "te2", "td", "to1", "to2", "tg"]
               + ["a%d" % r for r in range(N)] + ["y%d" % q for q in range(NQ)])
 
@@ -66,6 +66,29 @@ def _mask_of(bits):
     for b in bits:
         m |= 1 << b
     return m
+
+
+def _rounds(n, far_pair):
+    free = set((i, j) for i in range(n) for j in range(n) if i != j)
+    back = []
+
+    def search(i, used, p, cost, best):
+        if best[0] is not None and cost >= best[0]:
+            return
+        if i == n:
+            best[0], best[1] = cost, list(p)
+            return
+        for j in range(n):
+            if j not in used and (i, j) in free:
+                search(i + 1, used | {j}, p + [j], cost + (1 if far_pair(i, j) else 0), best)
+
+    for _ in range(n - 1):
+        best = [None, None]
+        search(0, frozenset(), [], 0, best)
+        back.append(best[1])
+        for i in range(n):
+            free.discard((i, best[1][i]))
+    return back[::-1]
 
 
 def rank_program(g, core, T, topo):
@@ -89,14 +112,17 @@ def rank_program(g, core, T, topo):
     def same_die(chip_no, die_no):
         return [c for c in cores if topo.chip(c) == chip_no and topo.die(c) == die_no][0]
 
-    def hops(c):
-        a, b = topo.chip(core), topo.chip(c)
+    def chip_hops(a, b):
         if a == b:
             return 0
         return 1 if (topo.mates(a, b) or topo.same_plane(a, b)) else 2
 
-    outs = [same_die(chips[(ci + k) % nch], topo.die(core)) for k in range(1, nch)]
-    ins = [same_die(chips[(ci - k) % nch], topo.die(core)) for k in range(1, nch)]
+    def hops(c):
+        return chip_hops(topo.chip(core), topo.chip(c))
+
+    plan = _rounds(nch, lambda i, j: chip_hops(chips[i], chips[j]) > 1)
+    outs = [same_die(chips[p[ci]], topo.die(core)) for p in plan]
+    ins = [same_die(chips[p.index(ci)], topo.die(core)) for p in plan]
     others = sorted([c for c in cores if c != core], key=lambda c: -hops(c))
     for c in others:
         assert topo.may_write(core, c)
@@ -116,8 +142,8 @@ def rank_program(g, core, T, topo):
         return T.land[:, CAP * r:CAP * (r + 1)]
 
     SY.dma_start(T.kall[rank], T.keep[:]).then_inc(S.kd, 16)
-    SY.dma_start(T.kw[:], T.keep[:]).then_inc(S.kwl, 16)
-    SC.dma_start(T.xs[:], T.x[:]).then_inc(S.xl, 16)
+    SC.dma_start(T.kw[:], T.keep[:]).then_inc(S.kwl, 16)
+    SY.dma_start(T.xs[:], T.x[:]).then_inc(S.xl, 16)
 
     g.iota(T.qk[:], [[0, 8], [1, 16]], 0, -1, allow_small_or_imprecise_dtypes=True).then_inc(S.gq, 1)
     g.wait_ge(S.kd, 16)
@@ -144,23 +170,22 @@ def rank_program(g, core, T, topo):
     V.memset(T.z32[:], 0.0).then_inc(S.vm, 1)
     V.wait_ge(S.vm, 3)
     V.tensor_tensor_scan(T.c16f[:], T.m16[0:16, :], T.z32[:], 512.0, A.add, A.add).then_inc(S.vc0a, 1)
+    V.memset(T.on[:], 1.0).then_inc(S.von, 1)
     V.wait_ge(S.vc0a, 1)
     V.tensor_copy(T.c16[:], T.c16f[:]).then_inc(S.vc0b, 1)
     V.wait_ge(S.gq, 1)
-    V.tensor_copy(T.kcp[:, 0:1], T.qk[:, 15:16]).then_inc(S.vc1, 1)
-    V.tensor_scalar(T.eb[:], T.qk[:], 0.0, None, A.is_equal).then_inc(S.vc1, 1)
-    V.tensor_scalar(T.w3[:], T.qk[:], 0.0, -1.0, A.is_equal, A.mult).then_inc(S.vc1, 1)
+    V.tensor_scalar(T.uun[:], T.qk[:], 0.0, -1.0, A.is_gt, A.mult).then_inc(S.vc1, 1)
     V.tensor_scalar(T.e2[:], T.qk[:], 0.0, T.qk[:, 15:16], A.is_equal, A.mult).then_inc(S.vc1, 1)
-    V.tensor_scalar(T.uu[:], T.qk[:], 0.0, None, A.is_gt).then_inc(S.vc1, 1)
-    V.wait_ge(S.vc1, 5)
-    V.tensor_tensor(T.w1[:], T.uu[:], T.e2[:], A.subtract).then_inc(S.vc2, 1)
-    V.wait_ge(S.vc2, 1)
-    V.tensor_scalar(T.w2[:], T.w1[:], -1.0, 1.0, A.mult, A.add).then_inc(S.vc3, 1)
+    V.tensor_scalar(T.w3[:], T.qk[:], 0.0, -1.0, A.is_equal, A.mult).then_inc(S.vc1, 1)
+    V.tensor_scalar(T.eb[:], T.qk[:], 0.0, None, A.is_equal).then_inc(S.vc1, 1)
+    V.tensor_copy(T.kcp[:, 0:1], T.qk[:, 15:16]).then_inc(S.vc1, 1)
     V.wait_ge(S.vc0b, 1)
     V.wait_ge(S.kwl, 16)
     V.tensor_copy(T.kbp[:, 1:33], T.kw[:]).then_inc(S.vk, 1)
-    V.tensor_tensor(T.kcp[:, 1:33], T.kw[:], T.c16[:], A.mult).then_inc(S.vk, 1)
-    V.wait_ge(S.td, 4)
+    V.wait_ge(S.vk, 1)
+    V.tensor_tensor(T.dn[:], T.kbp[:, 0:32], T.kbp[:, 1:33], A.subtract).then_inc(S.vdn, 1)
+    V.tensor_tensor(T.kcp[:, 1:33], T.kw[:], T.c16[:], A.mult).then_inc(S.vk2, 1)
+    V.wait_ge(S.td, 5)
     V.tensor_tensor_scan(T.of[:], T.psd[:, 0:32], T.m16[:], 512.0, A.add, A.add).then_inc(S.vs1, 1)
     V.wait_ge(S.vs1, 1)
     V.tensor_copy(T.ou[:], T.of[:]).then_inc(S.vs2, 1)
@@ -200,12 +225,14 @@ def rank_program(g, core, T, topo):
 
     PE.wait_ge(S.vc1, 5)
     PE.matmul(T.pse[:, 0:128], T.eb[:], T.eb[:], True, True).then_inc(S.te1, 1)
-    PE.wait_ge(S.vc2, 1)
-    PE.wait_ge(S.vc3, 1)
+    PE.wait_ge(S.von, 1)
     PE.wait_ge(S.vm, 3)
-    PE.wait_ge(S.vk, 2)
-    PE.matmul(T.psd[:, 0:32], T.w1[:], T.kbp[:, 1:33], True, False).then_inc(S.td, 1)
-    PE.matmul(T.psd[:, 0:32], T.w2[:], T.kbp[:, 0:32], False, False).then_inc(S.td, 1)
+    PE.wait_ge(S.vk, 1)
+    PE.matmul(T.psd[:, 0:32], T.on[:], T.kbp[:, 0:32], True, False).then_inc(S.td, 1)
+    PE.wait_ge(S.vdn, 1)
+    PE.matmul(T.psd[:, 0:32], T.uun[:], T.dn[:], False, False).then_inc(S.td, 1)
+    PE.matmul(T.psd[:, 0:32], T.e2[:], T.dn[:], False, False).then_inc(S.td, 1)
+    PE.wait_ge(S.vk2, 1)
     PE.matmul(T.psd[:, 0:32], T.w3[:], T.kcp[:, 1:33], False, False).then_inc(S.td, 1)
     PE.matmul(T.psd[:, 0:32], T.eb[:], T.kcp[:, 0:32], False, True).then_inc(S.td, 1)
     PE.wait_ge(S.se, 1)
@@ -238,20 +265,18 @@ def rank_program(g, core, T, topo):
             q.wait_ge(S["a%d" % T.rank_of(c)], nfar)
         q.wait_ge(S.fw, nnear * (len(ins) + 1))
 
-    def src(p):
-        return T.land[:, 0:YW + ZW].indirect(T.gu[:, p * QW // 16:(p + 1) * QW // 16])
+    def src(a, b):
+        return T.land[:, 0:YW + ZW].indirect(T.gu[:, a // 16:b // 16])
 
     all_here(V)
     all_here(SC)
-    for p in range(NQ):
-        piece = T.ysb[:, p * QW:(p + 1) * QW]
-        if p % 2 == 0:
-            V.tensor_copy(piece, src(p)).then_inc(S["y%d" % p], 1)
-            SY.wait_ge(S["y%d" % p], 1)
-            SY.dma_start(T.y[:, p * QW:(p + 1) * QW], piece).then_inc(S.sts, 16)
-        else:
-            SC.activation(piece, src(p), CP).then_inc(S["y%d" % p], 1)
-            SC.wait_ge(S["y%d" % p], 1)
-            SC.dma_start(T.y[:, p * QW:(p + 1) * QW], piece).then_inc(S.stc, 16)
-    SY.wait_ge(S.sts, 16 * (NQ // 2))
-    SC.wait_ge(S.stc, 16 * (NQ // 2))
+    a = 0
+    for k, w in enumerate(RW):
+        V.tensor_copy(T.ysb[:, a:a + w], src(a, a + w)).then_inc(S["y%d" % (2 * k)], 1)
+        SC.activation(T.ysb[:, a + w:a + 2 * w], src(a + w, a + 2 * w), CP).then_inc(S["y%d" % (2 * k + 1)], 1)
+        SY.wait_ge(S["y%d" % (2 * k)], 1)
+        SY.wait_ge(S["y%d" % (2 * k + 1)], 1)
+        SY.dma_start(T.y[:, a:a + 2 * w], T.ysb[:, a:a + 2 * w]).then_inc(S.sts, 16)
+        a += 2 * w
+    assert a == YW
+    SY.wait_ge(S.sts, 16 * len(RW))

from concourse.bass import DstId, RemoteDMATransfer
from concourse.mybir import AluOpType, AxisListType, ActivationFunctionType

N, TC, CAP = 12, 512, 192
YW = N * CAP
ZW = 16
RW = [320, 512, 320]
NQ = 2 * len(RW)

SCRATCH = {
    "xs": ("sbuf", [128, TC], "bfloat16"),
    "cb": ("sbuf", [128, TC], "bfloat16"),
    "land": ("sbuf", [128, YW + ZW], "bfloat16"),
    "ysb": ("sbuf", [128, YW], "bfloat16"),
    "kall": ("dram", [N, 128, 4], "int32"),
    "kw": ("sbuf", [16, 32], "int32"),
    "fl": ("sbuf", [96, 64], "int32"),
    "ff": ("sbuf", [96, 64], "float32"),
    "nf": ("sbuf", [96, 1], "float32"),
    "nb": ("sbuf", [97, 1], "bfloat16"),
    "qk": ("sbuf", [16, 128], "bfloat16"),
    "z32": ("sbuf", [16, 32], "float32"),
    "c16f": ("sbuf", [16, 32], "float32"),
    "c16": ("sbuf", [16, 32], "int32"),
    "ip": ("sbuf", [16, 144], "float32"),
    "tv": ("sbuf", [96, 208], "bfloat16"),
    "eb": ("sbuf", [16, 128], "bfloat16"),
    "e32": ("sbuf", [16, 128], "float32"),
    "w3": ("sbuf", [16, 128], "bfloat16"),
    "e2": ("sbuf", [16, 128], "bfloat16"),
    "uun": ("sbuf", [16, 128], "bfloat16"),
    "on": ("sbuf", [16, 128], "bfloat16"),
    "kbp": ("sbuf", [16, 33], "bfloat16"),
    "dn": ("sbuf", [16, 32], "bfloat16"),
    "kcp": ("sbuf", [16, 33], "bfloat16"),
    "m16": ("sbuf", [128, 32], "float32"),
    "of": ("sbuf", [128, 32], "float32"),
    "ou": ("sbuf", [128, 32], "uint16"),
    "tall": ("sbuf", [97, 208], "bfloat16"),
    "tdd": ("sbuf", [97, 192], "bfloat16"),
    "eq": ("sbuf", [128, 128], "bfloat16"),
    "jw": ("sbuf", [128, 144], "float32"),
    "r0": ("sbuf", [128, 144], "bfloat16"),
    "r1": ("sbuf", [64, 144], "bfloat16"),
    "gu": ("sbuf", [128, 144], "uint16"),
    "psd": ("psum", [128, 512], "float32"),
    "pse": ("psum", [128, 512], "float32"),
    "psj": ("psum", [128, 512], "float32"),
    "pso": ("psum", [128, 512], "float32"),
    "pso2": ("psum", [128, 512], "float32"),
    "psg": ("psum", [128, 512], "float32"),
}
SEMAPHORES = (["kd", "kwl", "xl", "fld", "fa", "fw", "loc", "sts",
               "gq", "gj", "gt", "vm", "vc0a", "vc0b", "vc1", "von", "vdn", "vk", "vk2", "vs1", "vs2", "vsc", "vown",
               "vz", "vt1", "vt2", "vf1", "vf2", "vf3", "vr0", "vr1", "vg2", "se", "sq", "sj",
               "te1", "te2", "td", "to1", "to2", "tg"]
              + ["a%d" % r for r in range(N)] + ["y%d" % q for q in range(NQ)])


def _bits(mask):
    return [b for b in range(16) if (mask >> b) & 1]


def _mask_of(bits):
    m = 0
    for b in bits:
        m |= 1 << b
    return m


def _rounds(n, far_pair):
    free = set((i, j) for i in range(n) for j in range(n) if i != j)
    back = []

    def search(i, used, p, cost, best):
        if best[0] is not None and cost >= best[0]:
            return
        if i == n:
            best[0], best[1] = cost, list(p)
            return
        for j in range(n):
            if j not in used and (i, j) in free:
                search(i + 1, used | {j}, p + [j], cost + (1 if far_pair(i, j) else 0), best)

    for _ in range(n - 1):
        best = [None, None]
        search(0, frozenset(), [], 0, best)
        back.append(best[1])
        for i in range(n):
            free.discard((i, best[1][i]))
    return back[::-1]


def rank_program(g, core, T, topo):
    rank = T.rank_of(core)
    if rank is None:
        return
    S = T.sem
    V, PE, SC, SY = g.vector, g.tensor, g.scalar, g.sync
    A = AluOpType
    CP = ActivationFunctionType.Copy
    cores = list(T.cores)

    chips = []
    for c in cores:
        if topo.chip(c) not in chips:
            chips.append(topo.chip(c))
    nch = len(chips)
    ci = chips.index(topo.chip(core))
    sib = [c for c in cores if topo.chip(c) == topo.chip(core) and c != core][0]

    def same_die(chip_no, die_no):
        return [c for c in cores if topo.chip(c) == chip_no and topo.die(c) == die_no][0]

    def chip_hops(a, b):
        if a == b:
            return 0
        return 1 if (topo.mates(a, b) or topo.same_plane(a, b)) else 2

    def hops(c):
        return chip_hops(topo.chip(core), topo.chip(c))

    plan = _rounds(nch, lambda i, j: chip_hops(chips[i], chips[j]) > 1)
    outs = [same_die(chips[p[ci]], topo.die(core)) for p in plan]
    ins = [same_die(chips[p.index(ci)], topo.die(core)) for p in plan]
    others = sorted([c for c in cores if c != core], key=lambda c: -hops(c))
    for c in others:
        assert topo.may_write(core, c)
    far = topo.mask(core, sib)
    for c in outs:
        far &= topo.mask(core, c)
    near = topo.mask(core, sib) & ~far
    nfar, nnear = len(_bits(far)), len(_bits(near))
    fbits = _bits(far)[::2]
    nfb = len(fbits)

    def did(c):
        rid, pid, _ = topo.addr(c)
        return DstId(rid=rid, pnc=pid)

    def slot(r):
        return T.land[:, CAP * r:CAP * (r + 1)]

    SY.dma_start(T.kall[rank], T.keep[:]).then_inc(S.kd, 16)
    SC.dma_start(T.kw[:], T.keep[:]).then_inc(S.kwl, 16)
    SY.dma_start(T.xs[:], T.x[:]).then_inc(S.xl, 16)

    g.iota(T.qk[:], [[0, 8], [1, 16]], 0, -1, allow_small_or_imprecise_dtypes=True).then_inc(S.gq, 1)
    g.wait_ge(S.kd, 16)
    g.remote_dma_fused([RemoteDMATransfer(dst_ids=[did(c) for c in others[i::nfb]], dma_engine_mask=_mask_of([fbits[i]]),
                                          remote_sem=S.fa, srcs=[T.kall[rank]],
                                          dsts=[T.kall[rank] for c in others[i::nfb]])
                        for i in range(nfb)], local_sem=S.loc)
    g.iota(T.ip[:], [[16, 144]], 0, 1, allow_small_or_imprecise_dtypes=True).then_inc(S.gj, 1)
    g.iota(T.tv[:], [[8, 13], [0, 16]], 0, -1, allow_small_or_imprecise_dtypes=True).then_inc(S.gt, 1)
    g.wait_ge(S.vsc, 1)
    g.remote_dma_fused([RemoteDMATransfer(dst_ids=[did(c) for c in outs], dma_engine_mask=far,
                                          remote_sem=S["a%d" % rank],
                                          srcs=[T.cb[:, 0:CAP]], dsts=[slot(rank) for c in outs])], local_sem=S.loc)
    srid, spid, _ = topo.addr(sib)
    g.remote_dma(slot(rank), T.cb[:, 0:CAP], S.fw, S.loc, spid, srid, near)
    for c in ins:
        r = T.rank_of(c)
        g.wait_ge(S["a%d" % r], nfar)
        g.remote_dma(slot(r), slot(r), S.fw, S.loc, spid, srid, near)
    g.wait_ge(S.loc, nfb + nfar + nnear + nnear * len(ins))

    V.memset(T.kbp[:, 0:1], 0.0).then_inc(S.vm, 1)
    V.memset(T.m16[:], -16.0).then_inc(S.vm, 1)
    V.memset(T.z32[:], 0.0).then_inc(S.vm, 1)
    V.wait_ge(S.vm, 3)
    V.tensor_tensor_scan(T.c16f[:], T.m16[0:16, :], T.z32[:], 512.0, A.add, A.add).then_inc(S.vc0a, 1)
    V.memset(T.on[:], 1.0).then_inc(S.von, 1)
    V.wait_ge(S.vc0a, 1)
    V.tensor_copy(T.c16[:], T.c16f[:]).then_inc(S.vc0b, 1)
    V.wait_ge(S.gq, 1)
    V.tensor_scalar(T.uun[:], T.qk[:], 0.0, -1.0, A.is_gt, A.mult).then_inc(S.vc1, 1)
    V.tensor_scalar(T.e2[:], T.qk[:], 0.0, T.qk[:, 15:16], A.is_equal, A.mult).then_inc(S.vc1, 1)
    V.tensor_scalar(T.w3[:], T.qk[:], 0.0, -1.0, A.is_equal, A.mult).then_inc(S.vc1, 1)
    V.tensor_scalar(T.eb[:], T.qk[:], 0.0, None, A.is_equal).then_inc(S.vc1, 1)
    V.tensor_copy(T.kcp[:, 0:1], T.qk[:, 15:16]).then_inc(S.vc1, 1)
    V.wait_ge(S.vc0b, 1)
    V.wait_ge(S.kwl, 16)
    V.tensor_copy(T.kbp[:, 1:33], T.kw[:]).then_inc(S.vk, 1)
    V.wait_ge(S.vk, 1)
    V.tensor_tensor(T.dn[:], T.kbp[:, 0:32], T.kbp[:, 1:33], A.subtract).then_inc(S.vdn, 1)
    V.tensor_tensor(T.kcp[:, 1:33], T.kw[:], T.c16[:], A.mult).then_inc(S.vk2, 1)
    V.wait_ge(S.td, 5)
    V.tensor_tensor_scan(T.of[:], T.psd[:, 0:32], T.m16[:], 512.0, A.add, A.add).then_inc(S.vs1, 1)
    V.wait_ge(S.vs1, 1)
    V.tensor_copy(T.ou[:], T.of[:]).then_inc(S.vs2, 1)
    V.wait_ge(S.vs2, 1)
    V.wait_ge(S.xl, 16)
    V.tensor_copy(T.cb[:, 0:TC].indirect(T.ou[:, 0:32]), T.xs[:]).then_inc(S.vsc, 1)
    V.memset(T.land[:, YW:YW + ZW], 0.0).then_inc(S.vz, 1)
    V.memset(T.nb[96:97, 0:1], 1.0).then_inc(S.vz, 1)
    V.memset(T.tall[96:97, :], 0.0).then_inc(S.vz, 1)
    V.memset(T.tdd[96:97, :], 192.0).then_inc(S.vz, 1)
    V.wait_ge(S.gt, 1)
    V.tensor_scalar(T.tall[0:96, :], T.tv[:], 0.0, None, A.is_gt).then_inc(S.vt1, 1)
    V.wait_ge(S.vt1, 1)
    V.tensor_tensor(T.tdd[0:96, :], T.tall[0:96, 0:192], T.tall[0:96, 16:208], A.subtract).then_inc(S.vt2, 1)
    V.wait_ge(S.fld, 16)
    V.tensor_copy(T.ff[:], T.fl[:]).then_inc(S.vf1, 1)
    V.wait_ge(S.vf1, 1)
    V.tensor_reduce(T.nf[:], T.ff[:], AxisListType.X, A.add).then_inc(S.vf2, 1)
    V.wait_ge(S.vf2, 1)
    V.tensor_copy(T.nb[0:96, 0:1], T.nf[:]).then_inc(S.vf3, 1)
    V.wait_ge(S.sj, 1)
    V.wait_ge(S.to1, 2)
    V.tensor_scalar(T.r0[:], T.jw[:], T.pso[:, 0:1], T.pso[:, 1:2], A.is_ge, A.mult).then_inc(S.vr0, 1)
    V.wait_ge(S.to2, 2)
    V.tensor_scalar(T.r1[:], T.jw[0:64, :], T.pso2[0:64, 0:1], T.pso2[0:64, 1:2], A.is_ge, A.mult).then_inc(S.vr1, 1)
    V.wait_ge(S.tg, 3)
    V.tensor_scalar(T.gu[:], T.psg[:, 0:144], float(YW), None, A.min).then_inc(S.vg2, 1)

    SC.wait_ge(S.vc1, 5)
    SC.activation(T.e32[:], T.eb[:], CP).then_inc(S.se, 1)
    SC.wait_ge(S.te1, 1)
    SC.activation(T.eq[:], T.pse[:, 0:128], CP).then_inc(S.sq, 1)
    SC.wait_ge(S.te2, 1)
    SC.activation(T.jw[:], T.psj[:, 0:144], CP).then_inc(S.sj, 1)
    SC.wait_ge(S.vsc, 1)
    SC.activation(slot(rank), T.cb[:, 0:CAP], CP).then_inc(S.vown, 1)

    PE.wait_ge(S.vc1, 5)
    PE.matmul(T.pse[:, 0:128], T.eb[:], T.eb[:], True, True).then_inc(S.te1, 1)
    PE.wait_ge(S.von, 1)
    PE.wait_ge(S.vm, 3)
    PE.wait_ge(S.vk, 1)
    PE.matmul(T.psd[:, 0:32], T.on[:], T.kbp[:, 0:32], True, False).then_inc(S.td, 1)
    PE.wait_ge(S.vdn, 1)
    PE.matmul(T.psd[:, 0:32], T.uun[:], T.dn[:], False, False).then_inc(S.td, 1)
    PE.matmul(T.psd[:, 0:32], T.e2[:], T.dn[:], False, False).then_inc(S.td, 1)
    PE.wait_ge(S.vk2, 1)
    PE.matmul(T.psd[:, 0:32], T.w3[:], T.kcp[:, 1:33], False, False).then_inc(S.td, 1)
    PE.matmul(T.psd[:, 0:32], T.eb[:], T.kcp[:, 0:32], False, True).then_inc(S.td, 1)
    PE.wait_ge(S.se, 1)
    PE.wait_ge(S.gj, 1)
    PE.matmul(T.psj[:, 0:144], T.e32[:], T.ip[:], True, True).then_inc(S.te2, 1)
    PE.matmul(T.psg[:, 0:144], T.e32[:], T.ip[:], True, False).then_inc(S.tg, 1)
    PE.wait_ge(S.vz, 4)
    PE.wait_ge(S.vt1, 1)
    PE.wait_ge(S.vt2, 1)
    PE.wait_ge(S.vf3, 1)
    PE.matmul(T.pso[:, 0:1], T.tall[:, 16:144], T.nb[:], True, True).then_inc(S.to1, 1)
    PE.matmul(T.pso[:, 1:2], T.tdd[:, 0:128], T.nb[:], True, True).then_inc(S.to1, 1)
    PE.matmul(T.pso2[0:64, 0:1], T.tall[:, 144:208], T.nb[:], True, True).then_inc(S.to2, 1)
    PE.matmul(T.pso2[0:64, 1:2], T.tdd[:, 128:192], T.nb[:], True, True).then_inc(S.to2, 1)
    PE.wait_ge(S.sq, 1)
    PE.wait_ge(S.vr0, 1)
    PE.matmul(T.psg[:, 0:144], T.eq[:], T.r0[:], False, False).then_inc(S.tg, 1)
    PE.wait_ge(S.vr1, 1)
    PE.matmul(T.psg[:, 0:144], T.eq[0:64, :], T.r1[:], False, True).then_inc(S.tg, 1)

    SY.wait_ge(S.fa, len(others))
    SY.wait_ge(S.kd, 16)
    SY.dma_start(T.fl[:], T.kall[:]).then_inc(S.fld, 16)

    def all_here(q):
        q.wait_ge(S.vg2, 1)
        q.wait_ge(S.vown, 1)
        q.wait_ge(S.vz, 4)
        for c in ins:
            q.wait_ge(S["a%d" % T.rank_of(c)], nfar)
        q.wait_ge(S.fw, nnear * (len(ins) + 1))

    def src(a, b):
        return T.land[:, 0:YW + ZW].indirect(T.gu[:, a // 16:b // 16])

    all_here(V)
    all_here(SC)
    a = 0
    for k, w in enumerate(RW):
        V.tensor_copy(T.ysb[:, a:a + w], src(a, a + w)).then_inc(S["y%d" % (2 * k)], 1)
        SC.activation(T.ysb[:, a + w:a + 2 * w], src(a + w, a + 2 * w), CP).then_inc(S["y%d" % (2 * k + 1)], 1)
        SY.wait_ge(S["y%d" % (2 * k)], 1)
        SY.wait_ge(S["y%d" % (2 * k + 1)], 1)
        SY.dma_start(T.y[:, a:a + 2 * w], T.ysb[:, a:a + 2 * w]).then_inc(S.sts, 16)
        a += 2 * w
    assert a == YW
    SY.wait_ge(S.sts, 16 * len(RW))
